import numpy as np
import ml_dtypes


def mxq(x, axis, fmt="e4m3"):
    dtype, down = {"e4m3": (ml_dtypes.float8_e4m3fn, 7), "e5m2": (ml_dtypes.float8_e5m2, 14)}[fmt]
    v = np.moveaxis(np.asarray(x, np.float32).astype(ml_dtypes.bfloat16).astype(np.float64), axis, -1)
    blocks = v.reshape(v.shape[:-1] + (-1, 32))
    amax = np.abs(blocks).max(-1, keepdims=True)
    byte = np.maximum(np.where(amax > 0, np.frexp(amax)[1] - 1 + 127, 0) - down, 1)
    scale = np.exp2(byte - 127.0)
    codes = (blocks / scale).astype(np.float32).astype(dtype).astype(np.float64)
    return np.moveaxis((codes * scale).reshape(v.shape), -1, axis)


WIDE = False


def mx_kscale(k):
    if not WIDE:
        return np.ones(k)
    levels = np.array([10, -10, 5, -5, 0])
    if k % 512:
        return np.exp2(np.random.permutation(np.resize(levels, k // 32))).repeat(32)
    a = np.empty((k // 512, 16))
    for p in range(k // 512):
        a[p, :8] = np.random.permutation(np.resize(levels, 8))
        for g in range(8):
            far = levels[np.abs(levels - a[p, g]) >= 10]
            a[p, g + 8] = far[np.random.randint(len(far))]
    return np.exp2(a.ravel()).repeat(32)


def f64(x):
    return np.asarray(x).astype(np.float64)


def striped8(idx):
    return np.asarray(idx).reshape(8, -1, 16).transpose(0, 2, 1).reshape(128, -1).astype(np.uint16)


def unstriped8(offs):
    return offs.reshape(8, 16, -1).transpose(0, 2, 1).reshape(8, -1).astype(np.int64)


def pick8(x, idx, run):
    r = np.arange(len(x))
    return x[r[:, None], idx[r % (8 * run) // run]]


E2M1 = np.array([0.0, 0.5, 1.0, 1.5, 2.0, 3.0, 4.0, 6.0, -0.0, -0.5, -1.0, -1.5, -2.0, -3.0, -4.0, -6.0])


def pack_weight(w, fmt):
    k, n = w.shape
    w = f64(np.asarray(w, np.float32).astype(ml_dtypes.bfloat16)).reshape(k // 32, 32, n)
    amax = np.abs(w).max(1)
    if fmt == "e4m3":
        byte = np.frexp(amax)[1] - 1 + 127 - 7
    else:
        mant, ex = np.frexp(amax / 6.0)
        byte = np.where(mant > 0.5, ex, ex - 1) + 127
    byte = np.clip(np.where(amax > 0, byte, 1), 1, 254)
    scaled = (w * np.exp2(127.0 - byte)[:, None, :]).reshape(k, n).astype(np.float32)
    by_word = np.ascontiguousarray(scaled.reshape(k // 512, 128, 4, n).transpose(0, 1, 3, 2))
    if fmt == "e4m3":
        words = by_word.astype(ml_dtypes.float8_e4m3fn).view(np.uint8)
    else:
        c = by_word.astype(ml_dtypes.float4_e2m1fn).view(np.uint8) & 0xF
        words = (c[..., 0::2] | (c[..., 1::2] << 4)).reshape(k // 512, 128, 2 * n)
    return np.ascontiguousarray(words), np.ascontiguousarray(byte.astype(np.uint8).reshape(k // 512, 16, n))


def unpack_weight(words, scales, fmt):
    g, _, n = scales.shape
    words = np.ascontiguousarray(words).reshape(g, 128, n, -1)
    if fmt == "e4m3":
        vals = words.view(ml_dtypes.float8_e4m3fn).astype(np.float64)
    else:
        nib = np.empty((g, 128, n, 4), np.uint8)
        nib[..., 0::2] = words & 0xF
        nib[..., 1::2] = words >> 4
        vals = E2M1[nib]
    vals = vals * np.repeat(np.exp2(scales.astype(np.float64) - 127.0), 8, axis=1)[..., None]
    return vals.transpose(0, 1, 3, 2).reshape(g * 512, n)


D, T, I, Q = 512, 1024, 512, 128


def setup_inputs():
    n = np.random.standard_normal
    idx = np.stack([np.random.permutation(T)[:I] for _ in range(8)])
    idx2 = np.stack([np.random.permutation(T)[:I] for _ in range(8)])
    idx3 = np.stack([np.random.permutation(T)[:I] for _ in range(8)])
    idx4 = np.stack([np.random.permutation(T)[:I] for _ in range(8)])
    fd = mx_kscale(D)
    keysp = pack_weight(n((D, T)) / fd[:, None], "e2m1")
    return {
        "query": (n((D, Q)) * 1.0 / np.sqrt(D) * fd[:, None]).astype(np.float32),
        "keys_words": keysp[0],
        "keys_scales": keysp[1],
        "old": (1.0 * n((Q, T))).astype(np.float32),
        "offs": striped8(idx),
        "offs2": striped8(idx2),
        "offs3": striped8(idx3),
        "offs4": striped8(idx4),
    }


def reference(query, keys_words, keys_scales, old, offs, offs2, offs3, offs4):
    idx = unstriped8(offs)
    idx2 = unstriped8(offs2)
    idx3 = unstriped8(offs3)
    idx4 = unstriped8(offs4)
    keysu = unpack_weight(keys_words, keys_scales, "e2m1")
    queryq = mxq(f64(query), 0, "e4m3")
    a = queryq.T @ keysu
    w = pick8(a, idx, 16) * pick8(a, idx2, 16)
    f1 = np.zeros((Q, T))
    f1[np.arange(Q)[:, None], idx[np.arange(Q) % 128 // 16]] = w
    f2 = f1 + f64(old)
    y = np.maximum(pick8(f2, idx3, 16), pick8(f2, idx4, 16))
    return y

@@ -1,0 +1,118 @@
+from contextlib import ExitStack
+
+import concourse.mybir as mybir
+
+D, T, I, Q = 512, 1024, 512, 128
+FLOPS = 2 * D * T * Q
+
+F32 = mybir.dt.float32
+BF16 = mybir.dt.bfloat16
+I32 = mybir.dt.int32
+U32 = mybir.dt.uint32
+U16 = mybir.dt.uint16
+U8 = mybir.dt.uint8
+FP8X4 = mybir.dt.float8_e4m3fn_x4
+FP4X4 = mybir.dt.float4_e2m1fn_x4
+ALU = mybir.AluOpType
+COPY = mybir.ActivationFunctionType.Copy
+
+P = 128
+PACK = 4
+LANES = 16
+WIDTHS = (256, 256, 256, 128, 128)
+CAST_SPLIT = 80
+HALF = I // 2
+
+
+def tile_attend_pairproduct_lean_throughtwo_heads_kernel(
+    tc, query, keys_words, keys_scales, old, offs, offs2, offs3, offs4, out
+):
+    nc = tc.nc
+    with ExitStack() as ctx:
+        lists = ctx.enter_context(tc.tile_pool(name="lists", bufs=1))
+        pool = ctx.enter_context(tc.tile_pool(name="work", bufs=1))
+        psum = ctx.enter_context(tc.psum_pool(name="psum", bufs=1))
+
+        q_raw = pool.tile([P, PACK, Q], F32, name="q_raw")
+        nc.sync.dma_start(out=q_raw[:], in_=query.rearrange("(p j) q -> p j q", j=PACK))
+
+        k_scales = pool.tile([P, T], U8, name="k_scales", align_bytes=64)
+        nc.vector.memset(k_scales[:].bitcast(I32), 0)
+        k_words = pool.tile([P, 2 * T], U8, name="k_words", align_bytes=64)
+        nc.sync.dma_start(out=k_words[:].bitcast(I32), in_=keys_words[0].bitcast(I32))
+        for quad in range(4):
+            queue = nc.scalar if quad < 2 else nc.sync
+            queue.dma_start(
+                out=k_scales[32 * quad : 32 * quad + 4, :].bitcast(I32),
+                in_=keys_scales[0, 4 * quad : 4 * quad + 4, :].bitcast(I32),
+            )
+
+        idx1 = lists.tile([P, I // LANES], U16, name="idx1")
+        nc.sync.dma_start(idx1[:], offs)
+        idx2 = lists.tile([P, I // LANES], U16, name="idx2")
+        nc.sync.dma_start(idx2[:], offs2)
+        old_sb = pool.tile([P, T], F32, name="old_sb")
+        nc.sync.dma_start(out=old_sb[:], in_=old)
+        idx3 = lists.tile([P, I // LANES], U16, name="idx3")
+        nc.sync.dma_start(idx3[:], offs3)
+        idx4 = lists.tile([P, I // LANES], U16, name="idx4")
+        nc.sync.dma_start(idx4[:], offs4)
+
+        placed = pool.tile([P, T], F32, name="placed")
+        nc.vector.memset(placed[:], 0.0)
+
+        q_grouped = pool.tile([P, Q, PACK], BF16, name="q_grouped", align_bytes=64)
+        q_by_column = q_raw[:].rearrange("p j q -> p q j")
+        nc.vector.tensor_copy(out=q_grouped[:, :CAST_SPLIT, :], in_=q_by_column[:, :CAST_SPLIT, :])
+        nc.scalar.copy(out=q_grouped[:, CAST_SPLIT:, :], in_=q_by_column[:, CAST_SPLIT:, :])
+        q_codes = pool.tile([P, Q], U32, name="q_codes", align_bytes=64)
+        q_scales = pool.tile([P, Q], U8, name="q_scales", align_bytes=64)
+        nc.vector.quantize_mx(
+            out=q_codes[:].bitcast(FP8X4),
+            scales=q_scales[:],
+            in_=q_grouped[:].rearrange("p q j -> p (q j)"),
+        )
+
+        scores = pool.tile([P, T], F32, name="scores")
+        for c, width in enumerate(WIDTHS):
+            start = sum(WIDTHS[:c])
+            cols = slice(start, start + width)
+            bank = psum.tile([P, width], F32, name=f"bank{c}")
+            nc.tensor.matmul_mx(
+                out=bank[:],
+                lhsT=q_codes[:].bitcast(FP8X4),
+                lhsT_scale=q_scales[:],
+                rhs=k_words[:, 2 * start : 2 * (start + width)].bitcast(FP4X4),
+                rhs_scale=k_scales[:, cols],
+                start=True,
+                stop=True,
+            )
+            if c % 2 == 0:
+                nc.scalar.copy(out=scores[:, cols], in_=bank[:])
+            else:
+                nc.vector.tensor_copy(out=scores[:, cols], in_=bank[:])
+
+        def half(idx, h):
+            return idx[:, h * HALF // LANES : (h + 1) * HALF // LANES]
+
+        left = [pool.tile([P, HALF], F32, name=f"left{h}") for h in range(2)]
+        right = [pool.tile([P, HALF], F32, name=f"right{h}") for h in range(2)]
+        nc.scalar.activation(left[0][:], scores[:].indirect(half(idx1, 0)), COPY)
+        nc.vector.tensor_copy(right[0][:], scores[:].indirect(half(idx2, 0)))
+        nc.scalar.activation(left[1][:], scores[:].indirect(half(idx1, 1)), COPY)
+        nc.scalar.activation(right[1][:], scores[:].indirect(half(idx2, 1)), COPY)
+        for h in range(2):
+            nc.vector.tensor_tensor(placed[:].indirect(half(idx1, h)), left[h][:], right[h][:], ALU.mult)
+
+        totals = pool.tile([P, T], F32, name="totals")
+        nc.vector.tensor_tensor(totals[:], placed[:], old_sb[:], ALU.add)
+
+        first = [pool.tile([P, HALF], F32, name=f"first{h}") for h in range(2)]
+        second = [pool.tile([P, HALF], F32, name=f"second{h}") for h in range(2)]
+        for h in range(2):
+            nc.vector.tensor_copy(first[h][:], totals[:].indirect(half(idx3, h)))
+            nc.scalar.activation(second[h][:], totals[:].indirect(half(idx4, h)), COPY)
+        for h in range(2):
+            larger = pool.tile([P, HALF], F32, name=f"larger{h}")
+            nc.vector.tensor_tensor(larger[:], first[h][:], second[h][:], ALU.max)
+            nc.sync.dma_start(out=out[:, h * HALF : (h + 1) * HALF], in_=larger[:])

@@ -20,7 +20,7 @@ P = 128
 PACK = 4
 LANES = 16
 WIDTHS = (256, 256, 256, 128, 128)
-CAST_SPLIT = 80
+CAST_SPLIT = 22
 HALF = I // 2
 
 
@@ -41,8 +41,7 @@ def tile_attend_pairproduct_lean_throughtwo_heads_kernel(
         k_words = pool.tile([P, 2 * T], U8, name="k_words", align_bytes=64)
         nc.sync.dma_start(out=k_words[:].bitcast(I32), in_=keys_words[0].bitcast(I32))
         for quad in range(4):
-            queue = nc.scalar if quad < 2 else nc.sync
-            queue.dma_start(
+            nc.sync.dma_start(
                 out=k_scales[32 * quad : 32 * quad + 4, :].bitcast(I32),
                 in_=keys_scales[0, 4 * quad : 4 * quad + 4, :].bitcast(I32),
             )
@@ -62,9 +61,10 @@ def tile_attend_pairproduct_lean_throughtwo_heads_kernel(
         nc.vector.memset(placed[:], 0.0)
 
         q_grouped = pool.tile([P, Q, PACK], BF16, name="q_grouped", align_bytes=64)
-        q_by_column = q_raw[:].rearrange("p j q -> p q j")
-        nc.vector.tensor_copy(out=q_grouped[:, :CAST_SPLIT, :], in_=q_by_column[:, :CAST_SPLIT, :])
-        nc.scalar.copy(out=q_grouped[:, CAST_SPLIT:, :], in_=q_by_column[:, CAST_SPLIT:, :])
+        cast_out = q_grouped[:].rearrange("p (c i) j -> p c j i", i=4)
+        cast_in = q_raw[:].rearrange("p j (c i) -> p c j i", i=4)
+        nc.vector.tensor_copy(out=cast_out[:, :CAST_SPLIT], in_=cast_in[:, :CAST_SPLIT])
+        nc.scalar.copy(out=cast_out[:, CAST_SPLIT:], in_=cast_in[:, CAST_SPLIT:])
         q_codes = pool.tile([P, Q], U32, name="q_codes", align_bytes=64)
         q_scales = pool.tile([P, Q], U8, name="q_scales", align_bytes=64)
         nc.vector.quantize_mx(

@@ -38,13 +38,14 @@ def tile_attend_pairproduct_lean_throughtwo_heads_kernel(
 
         k_scales = pool.tile([P, T], U8, name="k_scales", align_bytes=64)
         nc.vector.memset(k_scales[:].bitcast(I32), 0)
-        k_words = pool.tile([P, 2 * T], U8, name="k_words", align_bytes=64)
-        nc.sync.dma_start(out=k_words[:].bitcast(I32), in_=keys_words[0].bitcast(I32))
+        k_words = [pool.tile([P, T], U8, name=f"k_words{h}", align_bytes=64) for h in range(2)]
+        nc.sync.dma_start(out=k_words[0][:].bitcast(I32), in_=keys_words[0, :, :T].bitcast(I32))
         for quad in range(4):
             nc.sync.dma_start(
                 out=k_scales[32 * quad : 32 * quad + 4, :].bitcast(I32),
                 in_=keys_scales[0, 4 * quad : 4 * quad + 4, :].bitcast(I32),
             )
+        nc.sync.dma_start(out=k_words[1][:].bitcast(I32), in_=keys_words[0, :, T:].bitcast(I32))
 
         idx1 = lists.tile([P, I // LANES], U16, name="idx1")
         nc.sync.dma_start(idx1[:], offs)
@@ -82,7 +83,7 @@ def tile_attend_pairproduct_lean_throughtwo_heads_kernel(
                 out=bank[:],
                 lhsT=q_codes[:].bitcast(FP8X4),
                 lhsT_scale=q_scales[:],
-                rhs=k_words[:, 2 * start : 2 * (start + width)].bitcast(FP4X4),
+                rhs=k_words[2 * start // T][:, 2 * start % T : 2 * start % T + 2 * width].bitcast(FP4X4),
                 rhs_scale=k_scales[:, cols],
                 start=True,
                 stop=True,

@@ -20,7 +20,6 @@ P = 128
 PACK = 4
 LANES = 16
 WIDTHS = (256, 256, 256, 128, 128)
-CAST_SPLIT = 22
 HALF = I // 2
 
 
@@ -41,7 +40,8 @@ def tile_attend_pairproduct_lean_throughtwo_heads_kernel(
         k_words = [pool.tile([P, T], U8, name=f"k_words{h}", align_bytes=64) for h in range(2)]
         nc.sync.dma_start(out=k_words[0][:].bitcast(I32), in_=keys_words[0, :, :T].bitcast(I32))
         for quad in range(4):
-            nc.sync.dma_start(
+            queue = nc.scalar if quad < 2 else nc.sync
+            queue.dma_start(
                 out=k_scales[32 * quad : 32 * quad + 4, :].bitcast(I32),
                 in_=keys_scales[0, 4 * quad : 4 * quad + 4, :].bitcast(I32),
             )
@@ -64,15 +64,17 @@ def tile_attend_pairproduct_lean_throughtwo_heads_kernel(
         q_grouped = pool.tile([P, Q, PACK], BF16, name="q_grouped", align_bytes=64)
         cast_out = q_grouped[:].rearrange("p (c i) j -> p c j i", i=4)
         cast_in = q_raw[:].rearrange("p j (c i) -> p c j i", i=4)
-        nc.vector.tensor_copy(out=cast_out[:, :CAST_SPLIT], in_=cast_in[:, :CAST_SPLIT])
-        nc.scalar.copy(out=cast_out[:, CAST_SPLIT:], in_=cast_in[:, CAST_SPLIT:])
+        nc.vector.tensor_copy(out=cast_out[:, :16], in_=cast_in[:, :16])
+        nc.vector.tensor_copy(out=cast_out[:, 16:], in_=cast_in[:, 16:])
         q_codes = pool.tile([P, Q], U32, name="q_codes", align_bytes=64)
         q_scales = pool.tile([P, Q], U8, name="q_scales", align_bytes=64)
-        nc.vector.quantize_mx(
-            out=q_codes[:].bitcast(FP8X4),
-            scales=q_scales[:],
-            in_=q_grouped[:].rearrange("p q j -> p (q j)"),
-        )
+        for h in range(2):
+            rows = slice(h * Q // 2, (h + 1) * Q // 2)
+            nc.vector.quantize_mx(
+                out=q_codes[:, rows].bitcast(FP8X4),
+                scales=q_scales[:, rows],
+                in_=q_grouped[:, rows, :].rearrange("p q j -> p (q j)"),
+            )
 
         scores = pool.tile([P, T], F32, name="scores")
         for c, width in enumerate(WIDTHS):

from contextlib import ExitStack

import concourse.mybir as mybir

D, T, I, Q = 512, 1024, 512, 128
FLOPS = 2 * D * T * Q

F32 = mybir.dt.float32
BF16 = mybir.dt.bfloat16
I32 = mybir.dt.int32
U32 = mybir.dt.uint32
U16 = mybir.dt.uint16
U8 = mybir.dt.uint8
FP8X4 = mybir.dt.float8_e4m3fn_x4
FP4X4 = mybir.dt.float4_e2m1fn_x4
ALU = mybir.AluOpType
COPY = mybir.ActivationFunctionType.Copy

P = 128
PACK = 4
LANES = 16
WIDTHS = (256, 256, 256, 128, 128)
HALF = I // 2


def tile_attend_pairproduct_lean_throughtwo_heads_kernel(
    tc, query, keys_words, keys_scales, old, offs, offs2, offs3, offs4, out
):
    nc = tc.nc
    with ExitStack() as ctx:
        lists = ctx.enter_context(tc.tile_pool(name="lists", bufs=1))
        pool = ctx.enter_context(tc.tile_pool(name="work", bufs=1))
        psum = ctx.enter_context(tc.psum_pool(name="psum", bufs=1))

        q_raw = pool.tile([P, PACK, Q], F32, name="q_raw")
        nc.sync.dma_start(out=q_raw[:], in_=query.rearrange("(p j) q -> p j q", j=PACK))

        k_scales = pool.tile([P, T], U8, name="k_scales", align_bytes=64)
        nc.vector.memset(k_scales[:].bitcast(I32), 0)
        k_words = [pool.tile([P, T], U8, name=f"k_words{h}", align_bytes=64) for h in range(2)]
        nc.sync.dma_start(out=k_words[0][:].bitcast(I32), in_=keys_words[0, :, :T].bitcast(I32))
        for quad in range(4):
            queue = nc.scalar if quad < 2 else nc.sync
            queue.dma_start(
                out=k_scales[32 * quad : 32 * quad + 4, :].bitcast(I32),
                in_=keys_scales[0, 4 * quad : 4 * quad + 4, :].bitcast(I32),
            )
        nc.sync.dma_start(out=k_words[1][:].bitcast(I32), in_=keys_words[0, :, T:].bitcast(I32))

        idx1 = lists.tile([P, I // LANES], U16, name="idx1")
        nc.sync.dma_start(idx1[:], offs)
        idx2 = lists.tile([P, I // LANES], U16, name="idx2")
        nc.sync.dma_start(idx2[:], offs2)
        old_sb = pool.tile([P, T], F32, name="old_sb")
        nc.sync.dma_start(out=old_sb[:], in_=old)
        idx3 = lists.tile([P, I // LANES], U16, name="idx3")
        nc.sync.dma_start(idx3[:], offs3)
        idx4 = lists.tile([P, I // LANES], U16, name="idx4")
        nc.sync.dma_start(idx4[:], offs4)

        placed = pool.tile([P, T], F32, name="placed")
        nc.vector.memset(placed[:], 0.0)

        q_grouped = pool.tile([P, Q, PACK], BF16, name="q_grouped", align_bytes=64)
        cast_out = q_grouped[:].rearrange("p (c i) j -> p c j i", i=4)
        cast_in = q_raw[:].rearrange("p j (c i) -> p c j i", i=4)
        nc.vector.tensor_copy(out=cast_out[:, :16], in_=cast_in[:, :16])
        nc.vector.tensor_copy(out=cast_out[:, 16:], in_=cast_in[:, 16:])
        q_codes = pool.tile([P, Q], U32, name="q_codes", align_bytes=64)
        q_scales = pool.tile([P, Q], U8, name="q_scales", align_bytes=64)
        for h in range(2):
            rows = slice(h * Q // 2, (h + 1) * Q // 2)
            nc.vector.quantize_mx(
                out=q_codes[:, rows].bitcast(FP8X4),
                scales=q_scales[:, rows],
                in_=q_grouped[:, rows, :].rearrange("p q j -> p (q j)"),
            )

        scores = pool.tile([P, T], F32, name="scores")
        for c, width in enumerate(WIDTHS):
            start = sum(WIDTHS[:c])
            cols = slice(start, start + width)
            bank = psum.tile([P, width], F32, name=f"bank{c}")
            nc.tensor.matmul_mx(
                out=bank[:],
                lhsT=q_codes[:].bitcast(FP8X4),
                lhsT_scale=q_scales[:],
                rhs=k_words[2 * start // T][:, 2 * start % T : 2 * start % T + 2 * width].bitcast(FP4X4),
                rhs_scale=k_scales[:, cols],
                start=True,
                stop=True,
            )
            if c % 2 == 0:
                nc.scalar.copy(out=scores[:, cols], in_=bank[:])
            else:
                nc.vector.tensor_copy(out=scores[:, cols], in_=bank[:])

        def half(idx, h):
            return idx[:, h * HALF // LANES : (h + 1) * HALF // LANES]

        left = [pool.tile([P, HALF], F32, name=f"left{h}") for h in range(2)]
        right = [pool.tile([P, HALF], F32, name=f"right{h}") for h in range(2)]
        nc.scalar.activation(left[0][:], scores[:].indirect(half(idx1, 0)), COPY)
        nc.vector.tensor_copy(right[0][:], scores[:].indirect(half(idx2, 0)))
        nc.scalar.activation(left[1][:], scores[:].indirect(half(idx1, 1)), COPY)
        nc.scalar.activation(right[1][:], scores[:].indirect(half(idx2, 1)), COPY)
        for h in range(2):
            nc.vector.tensor_tensor(placed[:].indirect(half(idx1, h)), left[h][:], right[h][:], ALU.mult)

        totals = pool.tile([P, T], F32, name="totals")
        nc.vector.tensor_tensor(totals[:], placed[:], old_sb[:], ALU.add)

        first = [pool.tile([P, HALF], F32, name=f"first{h}") for h in range(2)]
        second = [pool.tile([P, HALF], F32, name=f"second{h}") for h in range(2)]
        for h in range(2):
            nc.vector.tensor_copy(first[h][:], totals[:].indirect(half(idx3, h)))
            nc.scalar.activation(second[h][:], totals[:].indirect(half(idx4, h)), COPY)
        for h in range(2):
            larger = pool.tile([P, HALF], F32, name=f"larger{h}")
            nc.vector.tensor_tensor(larger[:], first[h][:], second[h][:], ALU.max)
            nc.sync.dma_start(out=out[:, h * HALF : (h + 1) * HALF], in_=larger[:])
